import numpy as np
import ml_dtypes

BF16 = ml_dtypes.bfloat16


def bf(x):
    return np.asarray(x, np.float32).astype(BF16)


def f32(x):
    return np.asarray(x, np.float32)


def f64(x):
    return np.asarray(x).astype(np.float64)


def striped(idx):
    return np.tile(idx.reshape(-1, 16).T, (8, 1))


def rows(idx, k):
    return np.tile(idx, (k, 1))


def look(tab, idx):
    return np.take_along_axis(f64(tab), rows(idx, len(tab)), axis=1)


K, S, V, N, M = 512, 2048, 1024, 1024, 256


def setup_inputs():
    return {"tab": f32(np.random.standard_normal((2, K, S))), "y": f32(np.random.standard_normal((K, V))), "w": bf(np.random.standard_normal((K, M)) / np.sqrt(K)), "b": f32(0.5 * np.random.standard_normal((M, 1))), "offs": striped(np.random.permutation(S)[:N])}


def reference(tab, y, w, b, offs):
    idx = offs[:16].T.reshape(-1)
    x = (np.minimum(look(tab[0], idx), f64(y))) * (np.tanh(look(tab[1], idx)))
    return np.maximum(f64(w).T @ x + f64(b), 0.0)

@@ -1,0 +1,68 @@
+import concourse.mybir as mybir
+
+P = 128
+R, S, N, M = 512, 2048, 1024, 256
+BLOCKS = R // P
+HALVES = M // P
+PIECE = 512
+PIECES = N // PIECE
+LIST_COLUMNS = PIECE // 16
+FLOPS = 2 * R * M * N
+
+BF16, F32, U16 = mybir.dt.bfloat16, mybir.dt.float32, mybir.dt.uint16
+MIN, MULT, ADD, MAX = mybir.AluOpType.min, mybir.AluOpType.mult, mybir.AluOpType.add, mybir.AluOpType.max
+TANH, RELU = mybir.ActivationFunctionType.Tanh, mybir.ActivationFunctionType.Relu
+
+
+def tile_lookup_vg_mintanh_relu_kernel(tc, tab, y, w, b, offs, out):
+    nc = tc.nc
+    with (
+        tc.tile_pool(name="held", bufs=1) as held,
+        tc.psum_pool(name="sums", bufs=1) as sums,
+    ):
+        offsets = held.tile([P, N // 16], U16, name="offsets")
+        nc.sync.dma_start(offsets[:], offs)
+
+        bias = [held.tile([P, 1], F32, name="bias%d" % h) for h in range(HALVES)]
+        for h in range(HALVES):
+            nc.gpsimd.dma_start(bias[h][:], b[h * P : (h + 1) * P, :])
+
+        values = [held.tile([P, S], F32, name="values%d" % k) for k in range(BLOCKS)]
+        gates = [held.tile([P, S], F32, name="gates%d" % k) for k in range(BLOCKS)]
+        stream = [held.tile([P, N], F32, name="stream%d" % k) for k in range(BLOCKS)]
+        weights = held.tile([P, BLOCKS, M], BF16, name="weights")
+        for k in range(BLOCKS):
+            rows = slice(k * P, (k + 1) * P)
+            nc.sync.dma_start(values[k][:], tab[0, rows, :])
+            nc.sync.dma_start(stream[k][:], y[rows, :])
+            nc.sync.dma_start(gates[k][:], tab[1, rows, :])
+            if k == 0:
+                nc.sync.dma_start(weights[:], w.rearrange("(k p) m -> p k m", p=P))
+
+        acc = [[sums.tile([P, PIECE], F32, name="acc%d_%d" % (h, c)) for c in range(PIECES)] for h in range(HALVES)]
+        for k in range(BLOCKS):
+            for c in range(PIECES):
+                cols = slice(c * PIECE, (c + 1) * PIECE)
+                piece = offsets[:, c * LIST_COLUMNS : (c + 1) * LIST_COLUMNS]
+                smaller = held.tile([P, PIECE], F32, name="smaller%d_%d" % (k, c))
+                nc.vector.tensor_tensor(smaller[:], values[k][:].indirect(piece), stream[k][:, cols], MIN)
+                gate = held.tile([P, PIECE], F32, name="gate%d_%d" % (k, c))
+                nc.scalar.activation(gate[:], gates[k][:].indirect(piece), TANH)
+                x = held.tile([P, PIECE], BF16, name="x%d_%d" % (k, c))
+                nc.vector.tensor_tensor(x[:], smaller[:], gate[:], MULT)
+                for h in range(HALVES):
+                    nc.tensor.matmul(
+                        acc[h][c][:],
+                        weights[:, k, h * P : (h + 1) * P],
+                        x[:],
+                        start=(k == 0),
+                        stop=(k == BLOCKS - 1),
+                    )
+
+        for c in range(PIECES):
+            cols = slice(c * PIECE, (c + 1) * PIECE)
+            result = [held.tile([P, PIECE], F32, name="result%d_%d" % (h, c)) for h in range(HALVES)]
+            nc.scalar.activation(result[0][:], acc[0][c][:], RELU, bias=bias[0][:])
+            nc.vector.tensor_scalar(result[1][:], acc[1][c][:], bias[1][:], 0.0, ADD, MAX)
+            for h in range(HALVES):
+                nc.sync.dma_start(out[h * P : (h + 1) * P, cols], result[h][:])

@@ -1,10 +1,11 @@
 import concourse.mybir as mybir
+from concourse.masks import make_identity
 
 P = 128
 R, S, N, M = 512, 2048, 1024, 256
 BLOCKS = R // P
 HALVES = M // P
-PIECE = 512
+PIECE = 256
 PIECES = N // PIECE
 LIST_COLUMNS = PIECE // 16
 FLOPS = 2 * R * M * N
@@ -16,53 +17,62 @@ TANH, RELU = mybir.ActivationFunctionType.Tanh, mybir.ActivationFunctionType.Rel
 
 def tile_lookup_vg_mintanh_relu_kernel(tc, tab, y, w, b, offs, out):
     nc = tc.nc
-    with (
-        tc.tile_pool(name="held", bufs=1) as held,
-        tc.psum_pool(name="sums", bufs=1) as sums,
-    ):
+    tab_blocks = tab.rearrange("t (p k) s -> t k p s", k=BLOCKS)
+    y_blocks = y.rearrange("(p k) j -> k p j", k=BLOCKS)
+    with tc.tile_pool(name="held", bufs=1) as held:
         offsets = held.tile([P, N // 16], U16, name="offsets")
         nc.sync.dma_start(offsets[:], offs)
 
-        bias = [held.tile([P, 1], F32, name="bias%d" % h) for h in range(HALVES)]
-        for h in range(HALVES):
-            nc.gpsimd.dma_start(bias[h][:], b[h * P : (h + 1) * P, :])
+        identity = held.tile([P, P], F32, name="identity")
+        make_identity(nc, identity[:])
+        bias_rows = held.tile([P, P], F32, name="bias_rows")
+        nc.vector.memset(bias_rows[:], 0.0)
+        nc.sync.dma_start(bias_rows[0:HALVES, :], b.rearrange("(h p) o -> h (p o)", p=P))
+        bias = held.tile([P, HALVES], F32, name="bias")
+        with tc.psum_pool(name="turned", bufs=1) as turned:
+            bias_columns = turned.tile([P, P], F32, name="bias_columns")
+            nc.tensor.transpose(bias_columns[:], bias_rows[:], identity[:])
+            nc.vector.tensor_copy(bias[:], bias_columns[:, 0:HALVES])
 
         values = [held.tile([P, S], F32, name="values%d" % k) for k in range(BLOCKS)]
         gates = [held.tile([P, S], F32, name="gates%d" % k) for k in range(BLOCKS)]
         stream = [held.tile([P, N], F32, name="stream%d" % k) for k in range(BLOCKS)]
         weights = held.tile([P, BLOCKS, M], BF16, name="weights")
         for k in range(BLOCKS):
-            rows = slice(k * P, (k + 1) * P)
-            nc.sync.dma_start(values[k][:], tab[0, rows, :])
-            nc.sync.dma_start(stream[k][:], y[rows, :])
-            nc.sync.dma_start(gates[k][:], tab[1, rows, :])
+            early = N if k < BLOCKS - 1 else N - PIECE
+            nc.sync.dma_start(values[k][:], tab_blocks[0, k])
+            nc.sync.dma_start(stream[k][:, 0:early], y_blocks[k, :, 0:early])
+            nc.sync.dma_start(gates[k][:], tab_blocks[1, k])
             if k == 0:
-                nc.sync.dma_start(weights[:], w.rearrange("(k p) m -> p k m", p=P))
+                nc.sync.dma_start(weights[:], w.rearrange("(p k) m -> p k m", k=BLOCKS))
+            if early < N:
+                nc.sync.dma_start(stream[k][:, early:N], y_blocks[k, :, early:N])
 
-        acc = [[sums.tile([P, PIECE], F32, name="acc%d_%d" % (h, c)) for c in range(PIECES)] for h in range(HALVES)]
-        for k in range(BLOCKS):
+        with tc.psum_pool(name="sums", bufs=1) as sums:
+            acc = [[sums.tile([P, PIECE], F32, name="acc%d_%d" % (h, c)) for c in range(PIECES)] for h in range(HALVES)]
+            for k in range(BLOCKS):
+                for c in range(PIECES):
+                    cols = slice(c * PIECE, (c + 1) * PIECE)
+                    piece = offsets[:, c * LIST_COLUMNS : (c + 1) * LIST_COLUMNS]
+                    smaller = held.tile([P, PIECE], F32, name="smaller%d_%d" % (k, c))
+                    nc.vector.tensor_tensor(smaller[:], values[k][:].indirect(piece), stream[k][:, cols], MIN)
+                    gate = held.tile([P, PIECE], F32, name="gate%d_%d" % (k, c))
+                    nc.scalar.activation(gate[:], gates[k][:].indirect(piece), TANH)
+                    x = held.tile([P, PIECE], BF16, name="x%d_%d" % (k, c))
+                    nc.vector.tensor_tensor(x[:], smaller[:], gate[:], MULT)
+                    for h in range(HALVES):
+                        nc.tensor.matmul(
+                            acc[h][c][:],
+                            weights[:, k, h * P : (h + 1) * P],
+                            x[:],
+                            start=(k == 0),
+                            stop=(k == BLOCKS - 1),
+                        )
+
             for c in range(PIECES):
                 cols = slice(c * PIECE, (c + 1) * PIECE)
-                piece = offsets[:, c * LIST_COLUMNS : (c + 1) * LIST_COLUMNS]
-                smaller = held.tile([P, PIECE], F32, name="smaller%d_%d" % (k, c))
-                nc.vector.tensor_tensor(smaller[:], values[k][:].indirect(piece), stream[k][:, cols], MIN)
-                gate = held.tile([P, PIECE], F32, name="gate%d_%d" % (k, c))
-                nc.scalar.activation(gate[:], gates[k][:].indirect(piece), TANH)
-                x = held.tile([P, PIECE], BF16, name="x%d_%d" % (k, c))
-                nc.vector.tensor_tensor(x[:], smaller[:], gate[:], MULT)
+                result = [held.tile([P, PIECE], F32, name="result%d_%d" % (h, c)) for h in range(HALVES)]
+                nc.scalar.activation(result[0][:], acc[0][c][:], RELU, bias=bias[:, 0:1])
+                nc.vector.tensor_scalar(result[1][:], acc[1][c][:], bias[:, 1:2], 0.0, ADD, MAX)
                 for h in range(HALVES):
-                    nc.tensor.matmul(
-                        acc[h][c][:],
-                        weights[:, k, h * P : (h + 1) * P],
-                        x[:],
-                        start=(k == 0),
-                        stop=(k == BLOCKS - 1),
-                    )
-
-        for c in range(PIECES):
-            cols = slice(c * PIECE, (c + 1) * PIECE)
-            result = [held.tile([P, PIECE], F32, name="result%d_%d" % (h, c)) for h in range(HALVES)]
-            nc.scalar.activation(result[0][:], acc[0][c][:], RELU, bias=bias[0][:])
-            nc.vector.tensor_scalar(result[1][:], acc[1][c][:], bias[1][:], 0.0, ADD, MAX)
-            for h in range(HALVES):
-                nc.sync.dma_start(out[h * P : (h + 1) * P, cols], result[h][:])
+                    nc.sync.dma_start(out[h * P : (h + 1) * P, cols], result[h][:])

@@ -39,14 +39,14 @@ def tile_lookup_vg_mintanh_relu_kernel(tc, tab, y, w, b, offs, out):
         stream = [held.tile([P, N], F32, name="stream%d" % k) for k in range(BLOCKS)]
         weights = held.tile([P, BLOCKS, M], BF16, name="weights")
         for k in range(BLOCKS):
-            early = N if k < BLOCKS - 1 else N - PIECE
+            early = N if k < BLOCKS - 1 else N // 2
             nc.sync.dma_start(values[k][:], tab_blocks[0, k])
             nc.sync.dma_start(stream[k][:, 0:early], y_blocks[k, :, 0:early])
             nc.sync.dma_start(gates[k][:], tab_blocks[1, k])
             if k == 0:
                 nc.sync.dma_start(weights[:], w.rearrange("(p k) m -> p k m", k=BLOCKS))
-            if early < N:
-                nc.sync.dma_start(stream[k][:, early:N], y_blocks[k, :, early:N])
+            for late in range(early, N, PIECE):
+                nc.sync.dma_start(stream[k][:, late : late + PIECE], y_blocks[k, :, late : late + PIECE])
 
         with tc.psum_pool(name="sums", bufs=1) as sums:
             acc = [[sums.tile([P, PIECE], F32, name="acc%d_%d" % (h, c)) for c in range(PIECES)] for h in range(HALVES)]

@@ -39,14 +39,11 @@ def tile_lookup_vg_mintanh_relu_kernel(tc, tab, y, w, b, offs, out):
         stream = [held.tile([P, N], F32, name="stream%d" % k) for k in range(BLOCKS)]
         weights = held.tile([P, BLOCKS, M], BF16, name="weights")
         for k in range(BLOCKS):
-            early = N if k < BLOCKS - 1 else N // 2
             nc.sync.dma_start(values[k][:], tab_blocks[0, k])
-            nc.sync.dma_start(stream[k][:, 0:early], y_blocks[k, :, 0:early])
+            nc.sync.dma_start(stream[k][:], y_blocks[k])
             nc.sync.dma_start(gates[k][:], tab_blocks[1, k])
             if k == 0:
                 nc.sync.dma_start(weights[:], w.rearrange("(p k) m -> p k m", k=BLOCKS))
-            for late in range(early, N, PIECE):
-                nc.sync.dma_start(stream[k][:, late : late + PIECE], y_blocks[k, :, late : late + PIECE])
 
         with tc.psum_pool(name="sums", bufs=1) as sums:
             acc = [[sums.tile([P, PIECE], F32, name="acc%d_%d" % (h, c)) for c in range(PIECES)] for h in range(HALVES)]

@@ -18,7 +18,8 @@ TANH, RELU = mybir.ActivationFunctionType.Tanh, mybir.ActivationFunctionType.Rel
 def tile_lookup_vg_mintanh_relu_kernel(tc, tab, y, w, b, offs, out):
     nc = tc.nc
     tab_blocks = tab.rearrange("t (p k) s -> t k p s", k=BLOCKS)
-    y_blocks = y.rearrange("(p k) j -> k p j", k=BLOCKS)
+    y_runs = y.rearrange("(p k) j -> p (k j)", k=BLOCKS)
+    w_runs = w.rearrange("(p k) m -> p (k m)", k=BLOCKS)
     with tc.tile_pool(name="held", bufs=1) as held:
         offsets = held.tile([P, N // 16], U16, name="offsets")
         nc.sync.dma_start(offsets[:], offs)
@@ -36,23 +37,26 @@ def tile_lookup_vg_mintanh_relu_kernel(tc, tab, y, w, b, offs, out):
 
         values = [held.tile([P, S], F32, name="values%d" % k) for k in range(BLOCKS)]
         gates = [held.tile([P, S], F32, name="gates%d" % k) for k in range(BLOCKS)]
-        stream = [held.tile([P, N], F32, name="stream%d" % k) for k in range(BLOCKS)]
-        weights = held.tile([P, BLOCKS, M], BF16, name="weights")
+        stream = held.tile([P, BLOCKS * N], F32, name="stream")
+        weights = held.tile([P, BLOCKS * M], BF16, name="weights")
+        early = BLOCKS * N - PIECE
         for k in range(BLOCKS):
             nc.sync.dma_start(values[k][:], tab_blocks[0, k])
-            nc.sync.dma_start(stream[k][:], y_blocks[k])
+            if k == 0:
+                nc.sync.dma_start(stream[:, :early], y_runs[:, :early])
             nc.sync.dma_start(gates[k][:], tab_blocks[1, k])
             if k == 0:
-                nc.sync.dma_start(weights[:], w.rearrange("(p k) m -> p k m", k=BLOCKS))
+                nc.sync.dma_start(weights[:], w_runs)
+        nc.sync.dma_start(stream[:, early:], y_runs[:, early:])
 
         with tc.psum_pool(name="sums", bufs=1) as sums:
             acc = [[sums.tile([P, PIECE], F32, name="acc%d_%d" % (h, c)) for c in range(PIECES)] for h in range(HALVES)]
             for k in range(BLOCKS):
                 for c in range(PIECES):
-                    cols = slice(c * PIECE, (c + 1) * PIECE)
+                    first = k * N + c * PIECE
                     piece = offsets[:, c * LIST_COLUMNS : (c + 1) * LIST_COLUMNS]
                     smaller = held.tile([P, PIECE], F32, name="smaller%d_%d" % (k, c))
-                    nc.vector.tensor_tensor(smaller[:], values[k][:].indirect(piece), stream[k][:, cols], MIN)
+                    nc.vector.tensor_tensor(smaller[:], values[k][:].indirect(piece), stream[:, first : first + PIECE], MIN)
                     gate = held.tile([P, PIECE], F32, name="gate%d_%d" % (k, c))
                     nc.scalar.activation(gate[:], gates[k][:].indirect(piece), TANH)
                     x = held.tile([P, PIECE], BF16, name="x%d_%d" % (k, c))
@@ -60,7 +64,7 @@ def tile_lookup_vg_mintanh_relu_kernel(tc, tab, y, w, b, offs, out):
                     for h in range(HALVES):
                         nc.tensor.matmul(
                             acc[h][c][:],
-                            weights[:, k, h * P : (h + 1) * P],
+                            weights[:, k * M + h * P : k * M + (h + 1) * P],
                             x[:],
                             start=(k == 0),
                             stop=(k == BLOCKS - 1),

import concourse.mybir as mybir
from concourse.masks import make_identity

P = 128
R, S, N, M = 512, 2048, 1024, 256
BLOCKS = R // P
HALVES = M // P
PIECE = 256
PIECES = N // PIECE
LIST_COLUMNS = PIECE // 16
FLOPS = 2 * R * M * N

BF16, F32, U16 = mybir.dt.bfloat16, mybir.dt.float32, mybir.dt.uint16
MIN, MULT, ADD, MAX = mybir.AluOpType.min, mybir.AluOpType.mult, mybir.AluOpType.add, mybir.AluOpType.max
TANH, RELU = mybir.ActivationFunctionType.Tanh, mybir.ActivationFunctionType.Relu


def tile_lookup_vg_mintanh_relu_kernel(tc, tab, y, w, b, offs, out):
    nc = tc.nc
    tab_blocks = tab.rearrange("t (p k) s -> t k p s", k=BLOCKS)
    y_runs = y.rearrange("(p k) j -> p (k j)", k=BLOCKS)
    w_runs = w.rearrange("(p k) m -> p (k m)", k=BLOCKS)
    with tc.tile_pool(name="held", bufs=1) as held:
        offsets = held.tile([P, N // 16], U16, name="offsets")
        nc.sync.dma_start(offsets[:], offs)

        identity = held.tile([P, P], F32, name="identity")
        make_identity(nc, identity[:])
        bias_rows = held.tile([P, P], F32, name="bias_rows")
        nc.vector.memset(bias_rows[:], 0.0)
        nc.sync.dma_start(bias_rows[0:HALVES, :], b.rearrange("(h p) o -> h (p o)", p=P))
        bias = held.tile([P, HALVES], F32, name="bias")
        with tc.psum_pool(name="turned", bufs=1) as turned:
            bias_columns = turned.tile([P, P], F32, name="bias_columns")
            nc.tensor.transpose(bias_columns[:], bias_rows[:], identity[:])
            nc.vector.tensor_copy(bias[:], bias_columns[:, 0:HALVES])

        values = [held.tile([P, S], F32, name="values%d" % k) for k in range(BLOCKS)]
        gates = [held.tile([P, S], F32, name="gates%d" % k) for k in range(BLOCKS)]
        stream = held.tile([P, BLOCKS * N], F32, name="stream")
        weights = held.tile([P, BLOCKS * M], BF16, name="weights")
        early = BLOCKS * N - PIECE
        for k in range(BLOCKS):
            nc.sync.dma_start(values[k][:], tab_blocks[0, k])
            if k == 0:
                nc.sync.dma_start(stream[:, :early], y_runs[:, :early])
            nc.sync.dma_start(gates[k][:], tab_blocks[1, k])
            if k == 0:
                nc.sync.dma_start(weights[:], w_runs)
        nc.sync.dma_start(stream[:, early:], y_runs[:, early:])

        with tc.psum_pool(name="sums", bufs=1) as sums:
            acc = [[sums.tile([P, PIECE], F32, name="acc%d_%d" % (h, c)) for c in range(PIECES)] for h in range(HALVES)]
            for k in range(BLOCKS):
                for c in range(PIECES):
                    first = k * N + c * PIECE
                    piece = offsets[:, c * LIST_COLUMNS : (c + 1) * LIST_COLUMNS]
                    smaller = held.tile([P, PIECE], F32, name="smaller%d_%d" % (k, c))
                    nc.vector.tensor_tensor(smaller[:], values[k][:].indirect(piece), stream[:, first : first + PIECE], MIN)
                    gate = held.tile([P, PIECE], F32, name="gate%d_%d" % (k, c))
                    nc.scalar.activation(gate[:], gates[k][:].indirect(piece), TANH)
                    x = held.tile([P, PIECE], BF16, name="x%d_%d" % (k, c))
                    nc.vector.tensor_tensor(x[:], smaller[:], gate[:], MULT)
                    for h in range(HALVES):
                        nc.tensor.matmul(
                            acc[h][c][:],
                            weights[:, k * M + h * P : k * M + (h + 1) * P],
                            x[:],
                            start=(k == 0),
                            stop=(k == BLOCKS - 1),
                        )

            for c in range(PIECES):
                cols = slice(c * PIECE, (c + 1) * PIECE)
                result = [held.tile([P, PIECE], F32, name="result%d_%d" % (h, c)) for h in range(HALVES)]
                nc.scalar.activation(result[0][:], acc[0][c][:], RELU, bias=bias[:, 0:1])
                nc.vector.tensor_scalar(result[1][:], acc[1][c][:], bias[:, 1:2], 0.0, ADD, MAX)
                for h in range(HALVES):
                    nc.sync.dma_start(out[h * P : (h + 1) * P, cols], result[h][:])
